import numpy as np
import ml_dtypes


def mxq(x, axis, fmt="e4m3"):
    dtype, down = {"e4m3": (ml_dtypes.float8_e4m3fn, 7), "e5m2": (ml_dtypes.float8_e5m2, 14)}[fmt]
    v = np.moveaxis(np.asarray(x, np.float32).astype(ml_dtypes.bfloat16).astype(np.float64), axis, -1)
    blocks = v.reshape(v.shape[:-1] + (-1, 32))
    amax = np.abs(blocks).max(-1, keepdims=True)
    byte = np.maximum(np.where(amax > 0, np.frexp(amax)[1] - 1 + 127, 0) - down, 1)
    scale = np.exp2(byte - 127.0)
    codes = (blocks / scale).astype(np.float32).astype(dtype).astype(np.float64)
    return np.moveaxis((codes * scale).reshape(v.shape), -1, axis)


WIDE = False


def mx_kscale(k):
    if not WIDE:
        return np.ones(k)
    levels = np.array([10, -10, 5, -5, 0])
    if k % 512:
        return np.exp2(np.random.permutation(np.resize(levels, k // 32))).repeat(32)
    a = np.empty((k // 512, 16))
    for p in range(k // 512):
        a[p, :8] = np.random.permutation(np.resize(levels, 8))
        for g in range(8):
            far = levels[np.abs(levels - a[p, g]) >= 10]
            a[p, g + 8] = far[np.random.randint(len(far))]
    return np.exp2(a.ravel()).repeat(32)


def f64(x):
    return np.asarray(x).astype(np.float64)


def striped(idx):
    return np.tile(idx.reshape(-1, 16).T, (8, 1)).astype(np.uint16)


def unstriped(offs):
    return offs[:16].T.reshape(-1).astype(np.int64)


def striped8(idx):
    return np.concatenate([x.reshape(-1, 16).T for x in idx]).astype(np.uint16)


def runs(offs, k):
    lists = np.stack([offs[16 * r : 16 * r + 16].T.reshape(-1) for r in range(8)]).astype(np.int64)
    return lists[np.arange(k) % 512 // 64]


def pack_weight(w):
    k, n = w.shape
    w = f64(np.asarray(w, np.float32).astype(ml_dtypes.bfloat16)).reshape(k // 32, 32, n)
    amax = np.abs(w).max(1)
    byte = np.clip(np.where(amax > 0, np.frexp(amax)[1] - 1 + 127 - 7, 1), 1, 254)
    scaled = (w * np.exp2(127.0 - byte)[:, None, :]).reshape(k, n).astype(np.float32)
    words = np.ascontiguousarray(scaled.reshape(k // 512, 128, 4, n).transpose(0, 1, 3, 2)).astype(ml_dtypes.float8_e4m3fn).view(np.uint8)
    return words, np.ascontiguousarray(byte.astype(np.uint8).reshape(k // 512, 16, n))


def unpack_weight(words, scales):
    g, p, n, _ = words.shape
    vals = np.ascontiguousarray(words).view(ml_dtypes.float8_e4m3fn).astype(np.float64) * np.repeat(np.exp2(scales.astype(np.float64) - 127.0), 8, axis=1)[..., None]
    return vals.transpose(0, 1, 3, 2).reshape(g * 512, n)


E2M1 = np.array([0.0, 0.5, 1.0, 1.5, 2.0, 3.0, 4.0, 6.0, -0.0, -0.5, -1.0, -1.5, -2.0, -3.0, -4.0, -6.0])


def pack_fp4(w):
    k, n = w.shape
    w = f64(np.asarray(w, np.float32).astype(ml_dtypes.bfloat16)).reshape(k // 32, 32, n)
    amax = np.abs(w).max(1)
    mant, ex = np.frexp(amax / 6.0)
    byte = np.clip(np.where(amax > 0, np.where(mant > 0.5, ex, ex - 1) + 127, 1), 1, 254)
    scaled = (w * np.exp2(127.0 - byte)[:, None, :]).reshape(k, n).astype(np.float32)
    c = np.ascontiguousarray(scaled.reshape(k // 512, 128, 4, n).transpose(0, 1, 3, 2)).astype(ml_dtypes.float4_e2m1fn).view(np.uint8) & 0xF
    words = (c[..., 0::2] | (c[..., 1::2] << 4)).reshape(k // 512, 128, 2 * n)
    return np.ascontiguousarray(words), np.ascontiguousarray(byte.astype(np.uint8).reshape(k // 512, 16, n))


def unpack_fp4(words, scales):
    g, _, n = scales.shape
    words = np.ascontiguousarray(words).reshape(g, 128, n, 2)
    nib = np.empty((g, 128, n, 4), np.uint8)
    nib[..., 0::2] = words & 0xF
    nib[..., 1::2] = words >> 4
    vals = E2M1[nib] * np.repeat(np.exp2(scales.astype(np.float64) - 127.0), 8, axis=1)[..., None]
    return vals.transpose(0, 1, 3, 2).reshape(g * 512, n)


def sigmoid(v):
    return 1.0 / (1.0 + np.exp(-np.maximum(v, -700.0)))

def planes(y):
    n, m = y.shape
    v = y.astype(np.float32).astype(ml_dtypes.bfloat16).astype(np.float64).reshape(n // 32, 32, m)
    top = np.abs(v).max(1)
    byte = np.clip(np.where(top > 0, np.frexp(top)[1] - 1 + 127 - 7, 1), 1, 254)
    codes = (v * np.exp2(127.0 - byte)[:, None, :]).reshape(n, m).astype(np.float32).astype(ml_dtypes.float8_e4m3fn).view(np.uint8)
    words = codes.reshape(n // 512, 128, 4, m).transpose(0, 1, 3, 2)
    return np.ascontiguousarray(words), np.ascontiguousarray(byte.astype(np.uint8).reshape(n // 512, 16, m))


K, T, S, N, G, H, W = 512, 1024, 512, 512, 2048, 512, 256


def setup_inputs():
    n = np.random.standard_normal
    s = mx_kscale(K)[:, None]
    u = mx_kscale(S)
    packed_xT = pack_weight(n((K, T)) * s)
    packed_dT = pack_weight(n((K, G)) / s)
    packed_w1 = pack_fp4(n((H, N)) / np.sqrt(2 * H) / u[:, None])
    packed_w2 = pack_fp4(n((H, N)) / np.sqrt(2 * H) / u[:, None])
    perm = np.stack([np.random.permutation(S) for _ in range(8)])
    perm2 = np.random.permutation(S)
    return {
        "x_words": packed_xT[0],
        "x_scales": packed_xT[1],
        "d_words": packed_dT[0],
        "d_scales": packed_dT[1],
        "gn": (np.random.uniform(0.5, 1.5, (H, 1)) * u[:, None]).astype(np.float32),
        "gm": (np.random.uniform(0.5, 1.5, (H, 1)) * u[:, None]).astype(np.float32),
        "w1_words": packed_w1[0],
        "w1_scales": packed_w1[1],
        "w2_words": packed_w2[0],
        "w2_scales": packed_w2[1],
        "offs": striped(np.random.permutation(T)[:S]),
        "k1": striped8(np.random.randint(0, G, (8, H))),
        "two": striped(np.random.permutation(T)[:S]),
        "n1": striped8(perm[:, :W]),
        "n2": striped8(perm[:, W:]),
        "n3": striped(perm2[:W]),
        "n4": striped(perm2[W:]),
        "n5": striped(np.random.randint(0, S, G)),
    }


def reference(x_words, x_scales, d_words, d_scales, gn, gm, w1_words, w1_scales, w2_words, w2_scales, offs, k1, two, n1, n2, n3, n4, n5):
    d_k1 = unpack_weight(d_words, d_scales)[np.arange(K)[:, None], runs(k1, K)]
    xq = unpack_weight(x_words, x_scales)[:, unstriped(offs)]
    a = 0.0625 * (d_k1.T @ xq)
    pa = a[np.arange(H)[:, None], runs(n1, H)]
    pb = a[np.arange(H)[:, None], runs(n2, H)]
    rb = pa * pb
    ra = pa + pb
    ds = np.zeros((H, S))
    ds[np.arange(H)[:, None], runs(n1, H)] = ra
    dt = ds.copy()
    dt[np.arange(H)[:, None], runs(n2, H)] = rb
    z = f64(gn) * dt
    x_two = unpack_weight(x_words, x_scales)[:, unstriped(two)]
    b = 0.0625 * (d_k1.T @ x_two)
    pb2 = b[:, unstriped(n4)]
    pa2 = b[:, unstriped(n3)]
    rb2 = pb2 * sigmoid(pb2 - pa2)
    ra2 = pa2 * sigmoid(pa2 - pb2)
    ds2 = np.zeros((H, S))
    ds2[:, unstriped(n3)] = ra2
    dt2 = ds2.copy()
    dt2[:, unstriped(n4)] = rb2
    z2 = f64(gm) * dt2
    h = unpack_fp4(w1_words, w1_scales).T @ mxq(z, 0, "e4m3") + unpack_fp4(w2_words, w2_scales).T @ mxq(z2, 0, "e4m3")
    mb = h[:, unstriped(n5)]
    mn = mb.reshape(N, S, 4).min(axis=2)
    mx = mb.reshape(N, S, 4).max(axis=2)
    out_0 = np.maximum(h, mn) - (0.5 * mx)
    return (out_0,) + planes(out_0)

@@ -1,0 +1,290 @@
+from contextlib import ExitStack
+
+import concourse.mybir as mybir
+
+K, T, S, N, G, H, W = 512, 1024, 512, 512, 2048, 512, 256
+FLOPS = 2 * 512 * 512 * 512 * 4
+
+F32 = mybir.dt.float32
+BF16 = mybir.dt.bfloat16
+I32 = mybir.dt.int32
+U32 = mybir.dt.uint32
+U16 = mybir.dt.uint16
+U8 = mybir.dt.uint8
+FP8X4 = mybir.dt.float8_e4m3fn_x4
+FP4X4 = mybir.dt.float4_e2m1fn_x4
+ALU = mybir.AluOpType
+ACT = mybir.ActivationFunctionType
+
+P = 128
+PACK = 4
+CHUNKS = (256, 256)
+H_WINDOW = 1088
+
+
+def tile_picked_kjbondduelgmid_none_po_kernel(
+    tc, x_words, x_scales, d_words, d_scales, gn, gm, w1_words, w1_scales, w2_words, w2_scales,
+    offs, k1, two, n1, n2, n3, n4, n5, out_0, out_1, out_2,
+):
+    nc = tc.nc
+    with ExitStack() as ctx:
+        lists = ctx.enter_context(tc.tile_pool(name="lists", bufs=1))
+        keep = ctx.enter_context(tc.tile_pool(name="keep", bufs=1))
+        ring = ctx.enter_context(tc.tile_pool(name="ring", bufs=3))
+        psum = ctx.enter_context(tc.psum_pool(name="psum", bufs=8))
+
+        def load_list(src, name):
+            tile = lists.tile(list(src.shape), U16, name=name)
+            nc.sync.dma_start(tile[:], src)
+            return tile
+
+        d_sc_table = keep.tile([P, G], U8, name="d_sc_table")
+        nc.vector.memset(d_sc_table[:, 0 : 3 * G // 4].bitcast(I32), 0)
+        nc.gpsimd.memset(d_sc_table[:, 3 * G // 4 : G].bitcast(I32), 0)
+        nc.sync.dma_start(d_sc_table[0:P:8, :].bitcast(I32), d_scales[0].bitcast(I32))
+        x_sc_table = keep.tile([P, T], U8, name="x_sc_table", tag="early_1k", align_bytes=64)
+        nc.vector.memset(x_sc_table[:].bitcast(I32), 0)
+
+        k1_t = load_list(k1, "k1_t")
+        offs_t = load_list(offs, "offs_t")
+        n1_t = load_list(n1, "n1_t")
+        n2_t = load_list(n2, "n2_t")
+        x_table = keep.tile([P, T], I32, name="x_table")
+        nc.sync.dma_start(x_table[:], x_words[0].rearrange("p n t -> p (n t)").bitcast(I32))
+        n3_t = load_list(n3, "n3_t")
+        d_table = keep.tile([P, G], I32, name="d_table")
+        nc.sync.dma_start(d_table[:], d_words[0].rearrange("p n t -> p (n t)").bitcast(I32))
+        for q in range(4):
+            nc.sync.dma_start(x_sc_table[32 * q : 32 * q + 4, :].bitcast(I32), x_scales[0, 4 * q : 4 * q + 4, :].bitcast(I32))
+        two_t = load_list(two, "two_t")
+        n4_t = load_list(n4, "n4_t")
+
+        key_scales = keep.tile([P, H], U8, name="key_scales", align_bytes=64)
+        nc.vector.memset(key_scales[:].bitcast(I32), 0)
+
+        d_sc_dealt = keep.tile([P, H], U8, name="d_sc_dealt", tag="stage2", align_bytes=64)
+        halves = []
+        for half in range(2):
+            picked = keep.tile([P, H // 2], U8, name=f"d_sc_picked{half}", tag=f"stage{half}", align_bytes=64)
+            nc.vector.tensor_copy(picked[:], d_sc_table[:].indirect(k1_t[:, 16 * half : 16 * (half + 1)]))
+            halves.append(picked)
+        for half in range(2):
+            nc.vector.tensor_copy(
+                d_sc_dealt[:].rearrange("p (t m) -> p t m", t=PACK)[:, :, 64 * half : 64 * (half + 1)],
+                halves[half][:].rearrange("p (m t) -> p t m", t=PACK),
+            )
+        for q in range(4):
+            nc.scalar.dma_start(
+                key_scales[32 * q : 32 * q + 4, :].bitcast(I32), d_sc_dealt[32 * q : 32 * q + 32 : 8, :].bitcast(I32)
+            )
+
+        def pick_words(offsets, name, tag):
+            words = keep.tile([P, S], U32, name=name, tag=tag, align_bytes=64)
+            nc.vector.tensor_copy(words[:], x_table[:].bitcast(U32).indirect(offsets[:]))
+            return words
+
+        def pick_scales(offsets, name, tag):
+            scales = keep.tile([P, S], U8, name=name, tag=tag, align_bytes=64)
+            nc.vector.tensor_copy(scales[:], x_sc_table[:].indirect(offsets[:]))
+            return scales
+
+        xa_words = pick_words(offs_t, "xa_words", "xa_words")
+        d_picked = keep.tile([P, H], U32, name="d_picked", tag="stage1", align_bytes=64)
+        nc.vector.tensor_copy(d_picked[:], d_table[:].bitcast(U32).indirect(k1_t[:]))
+        key_words = keep.tile([P, H], I32, name="key_words", align_bytes=64)
+        nc.vector.tensor_copy(
+            key_words[:].rearrange("p (t m) -> p t m", t=PACK),
+            d_picked[:].bitcast(I32).rearrange("p (m t) -> p t m", t=PACK),
+        )
+        xa_scales = pick_scales(offs_t, "xa_scales", "stage0")
+
+        def score(words, scales, t):
+            acc = psum.tile([P, S], F32, name="acc")
+            cols = slice(P * t, P * (t + 1))
+            nc.tensor.matmul_mx(
+                acc[:], lhsT=key_words[:, cols].bitcast(FP8X4), lhsT_scale=key_scales[:, cols],
+                rhs=words[:].bitcast(FP8X4), rhs_scale=scales[:], start=True, stop=True,
+            )
+            return acc
+
+        a_acc = [score(xa_words, xa_scales, t) for t in range(PACK)]
+        xb_words = pick_words(two_t, "xb_words", "stage1")
+        xb_scales = pick_scales(two_t, "xb_scales", "stage2")
+        b_acc = [score(xb_words, xb_scales, t) for t in range(PACK)]
+
+        n5_t = load_list(n5, "n5_t")
+        w_sc_raw = keep.tile([P, 2, N], U8, name="w_sc_raw")
+        nc.gpsimd.memset(w_sc_raw[:].rearrange("p i n -> p (i n)").bitcast(I32), 0)
+        for i, scales in enumerate((w1_scales, w2_scales)):
+            nc.gpsimd.dma_start(w_sc_raw[0:P:8, i, :].bitcast(I32), scales[0].bitcast(I32))
+        w_raw = keep.tile([P, 2, 2 * N], U8, name="w_raw")
+        for i, words in enumerate((w1_words, w2_words)):
+            nc.gpsimd.dma_start(w_raw[:, i, :].bitcast(I32), words[0].bitcast(I32))
+        gains = keep.tile([P, 2, 8], F32, name="gains")
+        nc.gpsimd.dma_start(gains[:, 0, 0:PACK], gn.rearrange("(p t) o -> p (t o)", t=PACK))
+        nc.gpsimd.dma_start(gains[:, 1, 0:PACK], gm.rearrange("(p t) o -> p (t o)", t=PACK))
+        w_sc_dealt = keep.tile([P, 2, N], U8, name="w_sc_dealt")
+        nc.gpsimd.tensor_copy(
+            w_sc_dealt[:].rearrange("p i (t m) -> p i t m", t=PACK),
+            w_sc_raw[:].rearrange("p i (m t) -> p i t m", t=PACK),
+        )
+        w_codes = keep.tile([P, 2, 2 * N], U8, name="w_codes", align_bytes=64)
+        nc.scalar.copy(
+            w_codes[:].bitcast(U16).rearrange("p i (t m) -> p i t m", t=PACK),
+            w_raw[:].bitcast(U16).rearrange("p i (m t) -> p i t m", t=PACK),
+        )
+        w_sc = keep.tile([P, 2, N], U8, name="w_sc", tag="early_1k", align_bytes=64)
+        nc.gpsimd.memset(w_sc[:].rearrange("p i n -> p (i n)").bitcast(I32), 0)
+        for q in range(4):
+            nc.sync.dma_start(
+                w_sc[32 * q : 32 * q + 4].rearrange("p i n -> p (i n)").bitcast(I32),
+                w_sc_dealt[32 * q : 32 * q + 32 : 8].rearrange("p i n -> p (i n)").bitcast(I32),
+            )
+
+        z_pairs = [keep.tile([P, 2, S, 2], BF16, name=f"z_pairs{i}") for i in range(2)]
+
+        def round_rows(i, t, placed):
+            nc.vector.tensor_scalar(z_pairs[i][:, t // 2, :, t % 2], placed[:], gains[:, i, t : t + 1], None, ALU.mult)
+
+        def quantise_z(i):
+            woven = keep.tile([P, S * PACK], BF16, name=f"z_woven{i}", align_bytes=64)
+            nc.vector.tensor_copy(
+                woven[:].bitcast(F32).rearrange("p (c h) -> p c h", h=2),
+                z_pairs[i][:].rearrange("p h c e -> p (h c e)").bitcast(F32).rearrange("p (h c) -> p c h", h=2),
+            )
+            codes = keep.tile([P, S], U32, name=f"z_codes{i}", align_bytes=64)
+            scales = keep.tile([P, S], U8, name=f"z_scales{i}", align_bytes=64)
+            nc.vector.quantize_mx(codes[:].bitcast(FP8X4), scales[:], woven[:])
+            return codes, scales
+
+        def fetch(acc, first, second, name):
+            rows = ring.tile([P, S], F32, name=name + "_rows")
+            nc.scalar.activation(rows[:], acc[:], ACT.Copy, scale=0.0625)
+            return rows
+
+        def pick_pair(rows, first, second, name):
+            pair = ring.tile([P, 2, W], F32, name=name + "_pair", bufs=4)
+            nc.scalar.activation(pair[:, 0, :], rows[:].indirect(first[:]), ACT.Copy)
+            nc.scalar.activation(pair[:, 1, :], rows[:].indirect(second[:]), ACT.Copy)
+            return pair
+
+        def place_a(t, pair):
+            placed = ring.tile([P, S], F32, name="a_placed")
+            nc.vector.tensor_tensor(placed[:].indirect(n1_t[:]), pair[:, 0, :], pair[:, 1, :], ALU.add)
+            nc.vector.tensor_tensor(placed[:].indirect(n2_t[:]), pair[:, 0, :], pair[:, 1, :], ALU.mult)
+            return placed
+
+        def differ(pair):
+            diff = ring.tile([P, W], F32, name="diff", bufs=4)
+            nc.vector.tensor_tensor(diff[:], pair[:, 0, :], pair[:, 1, :], ALU.subtract)
+            return diff
+
+        def gates(diff):
+            gate = ring.tile([P, 2, W], F32, name="gate")
+            nc.scalar.activation(gate[:, 0, :], diff[:], ACT.Sigmoid)
+            nc.scalar.activation(gate[:, 1, :], diff[:], ACT.Sigmoid, scale=-1.0)
+            return gate
+
+        def gated_values(pair, gate):
+            gated = ring.tile([P, 2, W], F32, name="gated", bufs=4)
+            nc.vector.tensor_tensor(gated[:], pair[:], gate[:], ALU.mult)
+            return gated
+
+        def place_b_scalar(gated):
+            placed = ring.tile([P, S], F32, name="b_placed", bufs=4)
+            nc.scalar.activation(placed[:].indirect(n3_t[:]), gated[:, 0, :], ACT.Copy)
+            nc.scalar.activation(placed[:].indirect(n4_t[:]), gated[:, 1, :], ACT.Copy)
+            return placed
+
+        def place_b_vector(pair, gate):
+            placed = ring.tile([P, S], F32, name="b_placed", bufs=4)
+            nc.vector.tensor_tensor(placed[:].indirect(n3_t[:]), pair[:, 0, :], gate[:, 0, :], ALU.mult)
+            nc.vector.tensor_tensor(placed[:].indirect(n4_t[:]), pair[:, 1, :], gate[:, 1, :], ALU.mult)
+            return placed
+
+        acc = {"a": a_acc, "b": b_acc}
+        both = {"a": (n1_t, n2_t), "b": (n3_t, n4_t)}
+        turns = [("a", 0), ("a", 1), ("b", 0), ("b", 1), ("a", 2), ("b", 2), ("a", 3), ("b", 3)]
+        rows = fetch(acc["a"][0], None, None, "ab")
+        b_pair, diff, gate, gated, b_placed = {}, {}, {}, {}, {}
+        for n, (kind, t) in enumerate(turns):
+            now = rows
+            if n + 1 < len(turns):
+                rows = fetch(acc[turns[n + 1][0]][turns[n + 1][1]], None, None, "ab")
+            pair = pick_pair(now, *both[kind], kind)
+            if kind == "a":
+                round_rows(0, t, place_a(t, pair))
+            else:
+                b_pair[t] = pair
+                diff[t] = differ(pair)
+            if (kind, t) == ("b", 2):
+                for u in (0, 1):
+                    gated[u] = gated_values(b_pair[u], gates(diff[u]))
+        b_placed[0] = place_b_scalar(gated[0])
+        gated[2] = gated_values(b_pair[2], gates(diff[2]))
+        last_gate = gates(diff[3])
+        z_codes, z_scales = quantise_z(0)
+        last_placed = place_b_vector(b_pair[3], last_gate)
+        round_rows(1, 0, b_placed[0])
+        h_acc = [psum.tile([P, S], F32, name="acc") for t in range(PACK)]
+
+        def second_product(i, codes, scales):
+            for t in range(PACK):
+                nc.tensor.matmul_mx(
+                    h_acc[t][:], lhsT=w_codes[:, i, 2 * P * t : 2 * P * (t + 1)].bitcast(FP4X4),
+                    lhsT_scale=w_sc[:, i, P * t : P * (t + 1)],
+                    rhs=codes[:].bitcast(FP8X4), rhs_scale=scales[:], start=(i == 0), stop=(i == 1),
+                )
+
+        second_product(0, z_codes, z_scales)
+        for t in range(1, PACK - 1):
+            round_rows(1, t, place_b_scalar(gated[t]))
+        round_rows(1, PACK - 1, last_placed)
+        z2_codes, z2_scales = quantise_z(1)
+        second_product(1, z2_codes, z2_scales)
+
+        h_rows = [keep.tile([P, H_WINDOW], F32, name=f"h_rows{t}") for t in range(PACK)]
+        nc.scalar.copy(h_rows[0][:, 0:S], h_acc[0][:])
+        for t in range(1, PACK):
+            nc.vector.tensor_copy(h_rows[t][:, 0:S], h_acc[t][:])
+
+        out_rows = out_0.rearrange("(p t) j -> p t j", t=PACK)
+        out_words = out_1[0].rearrange("p n t -> p (n t)").bitcast(I32)
+        o_scales = keep.tile([P, S], U8, name="o_scales", align_bytes=64)
+        wovens = []
+        for c, CHUNK in enumerate(CHUNKS):
+            first = sum(CHUNKS[:c])
+            cols = slice(first, first + CHUNK)
+            result = keep.tile([P, PACK, CHUNK], F32, name=f"result{c}")
+            for t in range(PACK):
+                members = ring.tile([P, CHUNK, 4], F32, name="members", bufs=4)
+                lo, hi = first * 4 // 16, (first + CHUNK) * 4 // 16
+                nc.scalar.activation(
+                    members[:].rearrange("p j e -> p (j e)"), h_rows[t][:].indirect(n5_t[:, lo:hi]), ACT.Copy
+                )
+                lows = ring.tile([P, CHUNK, 2], F32, name="lows")
+                highs = ring.tile([P, CHUNK, 2], F32, name="highs")
+                nc.vector.tensor_tensor(lows[:], members[:, :, 0:2], members[:, :, 2:4], ALU.min)
+                nc.vector.tensor_tensor(highs[:], members[:, :, 0:2], members[:, :, 2:4], ALU.max)
+                mn = ring.tile([P, CHUNK], F32, name="mn")
+                mx = ring.tile([P, CHUNK], F32, name="mx")
+                nc.vector.tensor_tensor(mn[:], lows[:, :, 0], lows[:, :, 1], ALU.min)
+                nc.vector.tensor_tensor(mx[:], highs[:, :, 0], highs[:, :, 1], ALU.max)
+                top = ring.tile([P, CHUNK], F32, name="top")
+                nc.vector.tensor_tensor(top[:], mn[:], h_rows[t][:, cols], ALU.max)
+                nc.vector.scalar_tensor_tensor(result[:, t, :], mx[:], -0.5, top[:], ALU.mult, ALU.add)
+                nc.sync.dma_start(out_rows[:, t, cols], result[:, t, :])
+            woven = keep.tile([P, CHUNK * PACK], BF16, name=f"o_woven{c}", align_bytes=64)
+            weave = nc.vector.tensor_copy if c == len(CHUNKS) - 1 else nc.scalar.copy
+            weave(
+                woven[:].rearrange("p (c i t) -> p c t i", i=4, t=PACK),
+                result[:].rearrange("p t (c i) -> p c t i", i=4),
+            )
+            wovens.append((cols, woven))
+        for c, (cols, woven) in enumerate(wovens):
+            o_codes = keep.tile([P, CHUNKS[c]], U32, name=f"o_codes{c}", align_bytes=64)
+            nc.vector.quantize_mx(o_codes[:].bitcast(FP8X4), o_scales[:, cols], woven[:])
+            nc.sync.dma_start(out_words[:, cols], o_codes[:].bitcast(I32))
+        for q in range(4):
+            queue = nc.sync if q % 2 == 0 else nc.scalar
+            queue.dma_start(out_2[0, 4 * q : 4 * q + 4, :].bitcast(I32), o_scales[32 * q : 32 * q + 4, :].bitcast(I32))

@@ -3,7 +3,7 @@ from contextlib import ExitStack
 import concourse.mybir as mybir
 
 K, T, S, N, G, H, W = 512, 1024, 512, 512, 2048, 512, 256
-FLOPS = 2 * 512 * 512 * 512 * 4
+FLOPS = 2 * K * H * S * 2 + 2 * H * N * S * 2
 
 F32 = mybir.dt.float32
 BF16 = mybir.dt.bfloat16
@@ -18,8 +18,14 @@ ACT = mybir.ActivationFunctionType
 
 P = 128
 PACK = 4
-CHUNKS = (256, 256)
-H_WINDOW = 1088
+QUADS = 4
+BLOCK_PARTS = 8
+LIST_ROWS = 16
+MEMBERS = 4
+SCORE_SCALE = 0.0625
+PIECE = 256
+CHUNKS = (256, 128, 128)
+H_WINDOW = MEMBERS * PIECE + 64
 
 
 def tile_picked_kjbondduelgmid_none_po_kernel(
@@ -31,52 +37,65 @@ def tile_picked_kjbondduelgmid_none_po_kernel(
         lists = ctx.enter_context(tc.tile_pool(name="lists", bufs=1))
         keep = ctx.enter_context(tc.tile_pool(name="keep", bufs=1))
         ring = ctx.enter_context(tc.tile_pool(name="ring", bufs=3))
-        psum = ctx.enter_context(tc.psum_pool(name="psum", bufs=8))
+        psum = ctx.enter_context(tc.psum_pool(name="psum", bufs=2 * PACK))
 
         def load_list(src, name):
             tile = lists.tile(list(src.shape), U16, name=name)
             nc.sync.dma_start(tile[:], src)
             return tile
 
-        d_sc_table = keep.tile([P, G], U8, name="d_sc_table")
-        nc.vector.memset(d_sc_table[:, 0 : 3 * G // 4].bitcast(I32), 0)
-        nc.gpsimd.memset(d_sc_table[:, 3 * G // 4 : G].bitcast(I32), 0)
-        nc.sync.dma_start(d_sc_table[0:P:8, :].bitcast(I32), d_scales[0].bitcast(I32))
-        x_sc_table = keep.tile([P, T], U8, name="x_sc_table", tag="early_1k", align_bytes=64)
-        nc.vector.memset(x_sc_table[:].bitcast(I32), 0)
+        def deal(engine_copy, dealt, plain):
+            engine_copy(dealt, plain.rearrange("p (m t) -> p t m", t=PACK))
 
+        def place_scale_rows(plane, dealt, first):
+            for q in range(QUADS):
+                nc.sync.dma_start(
+                    plane[32 * q : 32 * q + PACK, :].bitcast(I32),
+                    dealt[32 * q + first : 32 * (q + 1) : BLOCK_PARTS, :].bitcast(I32),
+                )
+
+        d_sc_table = keep.tile([P, G], U8, name="d_sc_table")
+        nc.gpsimd.memset(d_sc_table[:].bitcast(I32), 0)
+        nc.sync.dma_start(d_sc_table[0:P:BLOCK_PARTS, :].bitcast(I32), d_scales[0].bitcast(I32))
+        x_sc_table = keep.tile([P, T], U8, name="x_sc_table")
+        nc.gpsimd.memset(x_sc_table[:].bitcast(I32), 0)
         k1_t = load_list(k1, "k1_t")
         offs_t = load_list(offs, "offs_t")
-        n1_t = load_list(n1, "n1_t")
-        n2_t = load_list(n2, "n2_t")
-        x_table = keep.tile([P, T], I32, name="x_table")
-        nc.sync.dma_start(x_table[:], x_words[0].rearrange("p n t -> p (n t)").bitcast(I32))
-        n3_t = load_list(n3, "n3_t")
         d_table = keep.tile([P, G], I32, name="d_table")
         nc.sync.dma_start(d_table[:], d_words[0].rearrange("p n t -> p (n t)").bitcast(I32))
-        for q in range(4):
-            nc.sync.dma_start(x_sc_table[32 * q : 32 * q + 4, :].bitcast(I32), x_scales[0, 4 * q : 4 * q + 4, :].bitcast(I32))
-        two_t = load_list(two, "two_t")
-        n4_t = load_list(n4, "n4_t")
+        for q in range(QUADS):
+            nc.sync.dma_start(
+                x_sc_table[32 * q : 32 * q + PACK, :].bitcast(I32), x_scales[0, PACK * q : PACK * (q + 1), :].bitcast(I32)
+            )
+        x_table = keep.tile([P, T], I32, name="x_table")
+        nc.sync.dma_start(x_table[:], x_words[0].rearrange("p n t -> p (n t)").bitcast(I32))
+        n1_t = load_list(n1, "n1_t")
+        n2_t = load_list(n2, "n2_t")
 
         key_scales = keep.tile([P, H], U8, name="key_scales", align_bytes=64)
         nc.vector.memset(key_scales[:].bitcast(I32), 0)
 
+        warm = keep.tile([P, 2, 8], F32, name="warm")
+        nc.vector.memset(warm[:, 0, :], 0.0)
+        nc.scalar.activation(warm[:, 1, :], warm[:, 0, :], ACT.Sigmoid)
+
         d_sc_dealt = keep.tile([P, H], U8, name="d_sc_dealt", tag="stage2", align_bytes=64)
-        halves = []
+        half_cols = H // 2 // LIST_ROWS
+        d_sc_halves = []
         for half in range(2):
             picked = keep.tile([P, H // 2], U8, name=f"d_sc_picked{half}", tag=f"stage{half}", align_bytes=64)
-            nc.vector.tensor_copy(picked[:], d_sc_table[:].indirect(k1_t[:, 16 * half : 16 * (half + 1)]))
-            halves.append(picked)
-        for half in range(2):
             nc.vector.tensor_copy(
-                d_sc_dealt[:].rearrange("p (t m) -> p t m", t=PACK)[:, :, 64 * half : 64 * (half + 1)],
-                halves[half][:].rearrange("p (m t) -> p t m", t=PACK),
+                picked[:], d_sc_table[:].indirect(k1_t[:, half_cols * half : half_cols * (half + 1)])
             )
-        for q in range(4):
-            nc.scalar.dma_start(
-                key_scales[32 * q : 32 * q + 4, :].bitcast(I32), d_sc_dealt[32 * q : 32 * q + 32 : 8, :].bitcast(I32)
-            )
+            d_sc_halves.append(picked)
+        for half in range(2):
+            places = d_sc_dealt[:].rearrange("p (t m) -> p t m", t=PACK)[:, :, P // 2 * half : P // 2 * (half + 1)]
+            deal(nc.vector.tensor_copy, places, d_sc_halves[half][:])
+        place_scale_rows(key_scales, d_sc_dealt, 0)
+        two_t = load_list(two, "two_t")
+        n3_t = load_list(n3, "n3_t")
+        n4_t = load_list(n4, "n4_t")
+        n5_t = load_list(n5, "n5_t")
 
         def pick_words(offsets, name, tag):
             words = keep.tile([P, S], U32, name=name, tag=tag, align_bytes=64)
@@ -88,15 +107,12 @@ def tile_picked_kjbondduelgmid_none_po_kernel(
             nc.vector.tensor_copy(scales[:], x_sc_table[:].indirect(offsets[:]))
             return scales
 
-        xa_words = pick_words(offs_t, "xa_words", "xa_words")
         d_picked = keep.tile([P, H], U32, name="d_picked", tag="stage1", align_bytes=64)
         nc.vector.tensor_copy(d_picked[:], d_table[:].bitcast(U32).indirect(k1_t[:]))
         key_words = keep.tile([P, H], I32, name="key_words", align_bytes=64)
-        nc.vector.tensor_copy(
-            key_words[:].rearrange("p (t m) -> p t m", t=PACK),
-            d_picked[:].bitcast(I32).rearrange("p (m t) -> p t m", t=PACK),
-        )
+        deal(nc.vector.tensor_copy, key_words[:].rearrange("p (t m) -> p t m", t=PACK), d_picked[:].bitcast(I32))
         xa_scales = pick_scales(offs_t, "xa_scales", "stage0")
+        xa_words = pick_words(offs_t, "xa_words", "xa_words")
 
         def score(words, scales, t):
             acc = psum.tile([P, S], F32, name="acc")
@@ -112,179 +128,216 @@ def tile_picked_kjbondduelgmid_none_po_kernel(
         xb_scales = pick_scales(two_t, "xb_scales", "stage2")
         b_acc = [score(xb_words, xb_scales, t) for t in range(PACK)]
 
-        n5_t = load_list(n5, "n5_t")
-        w_sc_raw = keep.tile([P, 2, N], U8, name="w_sc_raw")
-        nc.gpsimd.memset(w_sc_raw[:].rearrange("p i n -> p (i n)").bitcast(I32), 0)
-        for i, scales in enumerate((w1_scales, w2_scales)):
-            nc.gpsimd.dma_start(w_sc_raw[0:P:8, i, :].bitcast(I32), scales[0].bitcast(I32))
         w_raw = keep.tile([P, 2, 2 * N], U8, name="w_raw")
         for i, words in enumerate((w1_words, w2_words)):
             nc.gpsimd.dma_start(w_raw[:, i, :].bitcast(I32), words[0].bitcast(I32))
+        w_sc_raw = keep.tile([P, N], U8, name="w_sc_raw")
+        nc.vector.memset(w_sc_raw[:].bitcast(I32), 0)
+        for i, scales in enumerate((w1_scales, w2_scales)):
+            nc.gpsimd.dma_start(w_sc_raw[i:P:BLOCK_PARTS, :].bitcast(I32), scales[0].bitcast(I32))
         gains = keep.tile([P, 2, 8], F32, name="gains")
-        nc.gpsimd.dma_start(gains[:, 0, 0:PACK], gn.rearrange("(p t) o -> p (t o)", t=PACK))
-        nc.gpsimd.dma_start(gains[:, 1, 0:PACK], gm.rearrange("(p t) o -> p (t o)", t=PACK))
-        w_sc_dealt = keep.tile([P, 2, N], U8, name="w_sc_dealt")
-        nc.gpsimd.tensor_copy(
-            w_sc_dealt[:].rearrange("p i (t m) -> p i t m", t=PACK),
-            w_sc_raw[:].rearrange("p i (m t) -> p i t m", t=PACK),
-        )
+        for i, gain in enumerate((gn, gm)):
+            nc.gpsimd.dma_start(gains[:, i, 0:PACK], gain.rearrange("(p t) o -> p (t o)", t=PACK))
         w_codes = keep.tile([P, 2, 2 * N], U8, name="w_codes", align_bytes=64)
         nc.scalar.copy(
             w_codes[:].bitcast(U16).rearrange("p i (t m) -> p i t m", t=PACK),
             w_raw[:].bitcast(U16).rearrange("p i (m t) -> p i t m", t=PACK),
         )
-        w_sc = keep.tile([P, 2, N], U8, name="w_sc", tag="early_1k", align_bytes=64)
-        nc.gpsimd.memset(w_sc[:].rearrange("p i n -> p (i n)").bitcast(I32), 0)
-        for q in range(4):
-            nc.sync.dma_start(
-                w_sc[32 * q : 32 * q + 4].rearrange("p i n -> p (i n)").bitcast(I32),
-                w_sc_dealt[32 * q : 32 * q + 32 : 8].rearrange("p i n -> p (i n)").bitcast(I32),
-            )
 
-        z_pairs = [keep.tile([P, 2, S, 2], BF16, name=f"z_pairs{i}") for i in range(2)]
+        accs = {"a": a_acc, "b": b_acc}
+        pair_lists = {"a": (n1_t, n2_t), "b": (n3_t, n4_t)}
+        rows, pair, placed, diff, gated = {}, {}, {}, {}, {}
 
-        def round_rows(i, t, placed):
-            nc.vector.tensor_scalar(z_pairs[i][:, t // 2, :, t % 2], placed[:], gains[:, i, t : t + 1], None, ALU.mult)
-
-        def quantise_z(i):
-            woven = keep.tile([P, S * PACK], BF16, name=f"z_woven{i}", align_bytes=64)
-            nc.vector.tensor_copy(
-                woven[:].bitcast(F32).rearrange("p (c h) -> p c h", h=2),
-                z_pairs[i][:].rearrange("p h c e -> p (h c e)").bitcast(F32).rearrange("p (h c) -> p c h", h=2),
-            )
-            codes = keep.tile([P, S], U32, name=f"z_codes{i}", align_bytes=64)
-            scales = keep.tile([P, S], U8, name=f"z_scales{i}", align_bytes=64)
-            nc.vector.quantize_mx(codes[:].bitcast(FP8X4), scales[:], woven[:])
-            return codes, scales
-
-        def fetch(acc, first, second, name):
-            rows = ring.tile([P, S], F32, name=name + "_rows")
-            nc.scalar.activation(rows[:], acc[:], ACT.Copy, scale=0.0625)
-            return rows
-
-        def pick_pair(rows, first, second, name):
-            pair = ring.tile([P, 2, W], F32, name=name + "_pair", bufs=4)
-            nc.scalar.activation(pair[:, 0, :], rows[:].indirect(first[:]), ACT.Copy)
-            nc.scalar.activation(pair[:, 1, :], rows[:].indirect(second[:]), ACT.Copy)
-            return pair
-
-        def place_a(t, pair):
-            placed = ring.tile([P, S], F32, name="a_placed")
-            nc.vector.tensor_tensor(placed[:].indirect(n1_t[:]), pair[:, 0, :], pair[:, 1, :], ALU.add)
-            nc.vector.tensor_tensor(placed[:].indirect(n2_t[:]), pair[:, 0, :], pair[:, 1, :], ALU.mult)
-            return placed
-
-        def differ(pair):
-            diff = ring.tile([P, W], F32, name="diff", bufs=4)
-            nc.vector.tensor_tensor(diff[:], pair[:, 0, :], pair[:, 1, :], ALU.subtract)
-            return diff
-
-        def gates(diff):
-            gate = ring.tile([P, 2, W], F32, name="gate")
-            nc.scalar.activation(gate[:, 0, :], diff[:], ACT.Sigmoid)
-            nc.scalar.activation(gate[:, 1, :], diff[:], ACT.Sigmoid, scale=-1.0)
-            return gate
-
-        def gated_values(pair, gate):
-            gated = ring.tile([P, 2, W], F32, name="gated", bufs=4)
-            nc.vector.tensor_tensor(gated[:], pair[:], gate[:], ALU.mult)
-            return gated
-
-        def place_b_scalar(gated):
-            placed = ring.tile([P, S], F32, name="b_placed", bufs=4)
-            nc.scalar.activation(placed[:].indirect(n3_t[:]), gated[:, 0, :], ACT.Copy)
-            nc.scalar.activation(placed[:].indirect(n4_t[:]), gated[:, 1, :], ACT.Copy)
-            return placed
-
-        def place_b_vector(pair, gate):
-            placed = ring.tile([P, S], F32, name="b_placed", bufs=4)
-            nc.vector.tensor_tensor(placed[:].indirect(n3_t[:]), pair[:, 0, :], gate[:, 0, :], ALU.mult)
-            nc.vector.tensor_tensor(placed[:].indirect(n4_t[:]), pair[:, 1, :], gate[:, 1, :], ALU.mult)
-            return placed
-
-        acc = {"a": a_acc, "b": b_acc}
-        both = {"a": (n1_t, n2_t), "b": (n3_t, n4_t)}
-        turns = [("a", 0), ("a", 1), ("b", 0), ("b", 1), ("a", 2), ("b", 2), ("a", 3), ("b", 3)]
-        rows = fetch(acc["a"][0], None, None, "ab")
-        b_pair, diff, gate, gated, b_placed = {}, {}, {}, {}, {}
-        for n, (kind, t) in enumerate(turns):
-            now = rows
-            if n + 1 < len(turns):
-                rows = fetch(acc[turns[n + 1][0]][turns[n + 1][1]], None, None, "ab")
-            pair = pick_pair(now, *both[kind], kind)
-            if kind == "a":
-                round_rows(0, t, place_a(t, pair))
+        def empty_bank(kind, t):
+            name = f"rows_{kind}{t}"
+            rows[kind, t] = keep.tile([P, S], F32, name=name, tag=name)
+            if (kind, t) == ("a", 1):
+                nc.vector.tensor_scalar(rows[kind, t][:], accs[kind][t][:], SCORE_SCALE, None, ALU.mult)
             else:
-                b_pair[t] = pair
-                diff[t] = differ(pair)
-            if (kind, t) == ("b", 2):
-                for u in (0, 1):
-                    gated[u] = gated_values(b_pair[u], gates(diff[u]))
-        b_placed[0] = place_b_scalar(gated[0])
-        gated[2] = gated_values(b_pair[2], gates(diff[2]))
-        last_gate = gates(diff[3])
-        z_codes, z_scales = quantise_z(0)
-        last_placed = place_b_vector(b_pair[3], last_gate)
-        round_rows(1, 0, b_placed[0])
-        h_acc = [psum.tile([P, S], F32, name="acc") for t in range(PACK)]
+                nc.scalar.activation(rows[kind, t][:], accs[kind][t][:], ACT.Copy, scale=SCORE_SCALE)
 
-        def second_product(i, codes, scales):
-            for t in range(PACK):
-                nc.tensor.matmul_mx(
-                    h_acc[t][:], lhsT=w_codes[:, i, 2 * P * t : 2 * P * (t + 1)].bitcast(FP4X4),
-                    lhsT_scale=w_sc[:, i, P * t : P * (t + 1)],
-                    rhs=codes[:].bitcast(FP8X4), rhs_scale=scales[:], start=(i == 0), stop=(i == 1),
+        def pick_pair(kind, t):
+            name = f"pair_{kind}{t}"
+            pair[kind, t] = keep.tile([P, 2, W], F32, name=name, tag=name)
+            for side in range(2):
+                nc.scalar.activation(
+                    pair[kind, t][:, side, :], rows[kind, t][:].indirect(pair_lists[kind][side][:]), ACT.Copy
                 )
 
-        second_product(0, z_codes, z_scales)
-        for t in range(1, PACK - 1):
-            round_rows(1, t, place_b_scalar(gated[t]))
-        round_rows(1, PACK - 1, last_placed)
-        z2_codes, z2_scales = quantise_z(1)
-        second_product(1, z2_codes, z2_scales)
+        def place_sum(t):
+            placed["a", t] = keep.tile([P, S], F32, name=f"placed_a{t}", tag=f"placed_a{t}")
+            window, pa, pb = placed["a", t][:].indirect(n1_t[:]), pair["a", t][:, 0, :], pair["a", t][:, 1, :]
+            if t == 0:
+                nc.vector.tensor_tensor(window, pa, pb, ALU.add)
+            else:
+                total = ring.tile([P, W], F32, name="total")
+                nc.gpsimd.tensor_tensor(total[:], pa, pb, ALU.add)
+                nc.vector.tensor_copy(window, total[:])
 
-        h_rows = [keep.tile([P, H_WINDOW], F32, name=f"h_rows{t}") for t in range(PACK)]
-        nc.scalar.copy(h_rows[0][:, 0:S], h_acc[0][:])
+        def place_product(t):
+            tag = f"rows_a{t + 1}" if t % 2 == 0 else f"product{t}"
+            product = keep.tile([P, W], F32, name=f"product{t}", tag=tag)
+            nc.gpsimd.tensor_tensor(product[:], pair["a", t][:, 0, :], pair["a", t][:, 1, :], ALU.mult)
+            nc.vector.tensor_copy(placed["a", t][:].indirect(n2_t[:]), product[:])
+
+        def subtract(t):
+            diff[t] = keep.tile([P, W], F32, name=f"diff{t}", tag=f"diff{t}")
+            nc.gpsimd.tensor_tensor(diff[t][:], pair["b", t][:, 0, :], pair["b", t][:, 1, :], ALU.subtract)
+
+        def gate(t):
+            sigmoids = ring.tile([P, 2, W], F32, name="sigmoids")
+            for side, sign in enumerate((1.0, -1.0)):
+                nc.scalar.activation(sigmoids[:, side, :], diff[t][:], ACT.Sigmoid, scale=sign)
+            gated[t] = keep.tile([P, 2, W], F32, name=f"gated{t}")
+            nc.gpsimd.tensor_tensor(gated[t][:], pair["b", t][:], sigmoids[:], ALU.mult)
+
+        def place_gated(t, tag):
+            placed["b", t] = keep.tile([P, S], F32, name=f"placed_b{t}", tag=tag)
+            for side in range(2):
+                window = placed["b", t][:].indirect(pair_lists["b"][side][:])
+                if t % 2 == 0:
+                    nc.vector.tensor_copy(window, gated[t][:, side, :])
+                else:
+                    nc.scalar.activation(window, gated[t][:, side, :], ACT.Copy)
+
+        turns = [("a", 0), ("a", 1), ("b", 0), ("a", 2), ("a", 3), ("b", 1), ("b", 2), ("b", 3)]
+        for kind, t in turns:
+            empty_bank(kind, t)
+            pick_pair(kind, t)
+            if kind == "b":
+                subtract(t)
+                continue
+            place_sum(t)
+            if t % 2 == 1:
+                place_product(t - 1)
+                place_product(t)
+            if t == PACK - 1:
+                gate(0)
         for t in range(1, PACK):
-            nc.vector.tensor_copy(h_rows[t][:, 0:S], h_acc[t][:])
+            gate(t)
+        place_gated(0, f"product{PACK - 1}")
+        place_gated(2, "placed_b2")
+        place_gated(1, f"diff{PACK - 1}")
+        place_gated(3, "placed_b3")
+
+        w_sc_dealt = keep.tile([P, N], U8, name="w_sc_dealt", tag="rows_a0")
+        deal(nc.vector.tensor_copy, w_sc_dealt[:].rearrange("p (t m) -> p t m", t=PACK), w_sc_raw[:])
+        w_sc = keep.tile([P, 2, N], U8, name="w_sc", align_bytes=64)
+        nc.vector.memset(w_sc[:].rearrange("p i n -> p (i n)").bitcast(I32), 0)
+        for i in range(2):
+            place_scale_rows(w_sc[:, i, :], w_sc_dealt, i)
+
+        z_pairs = {}
+
+        def round_rows(engine, i, t, parts):
+            source = placed["ab"[i], t]
+            for part in range(parts):
+                cols = slice(part * S // parts, (part + 1) * S // parts)
+                rounded, gain = z_pairs[i][:, t // 2, cols, t % 2], gains[:, i, t : t + 1]
+                if engine == "scalar":
+                    nc.scalar.activation(rounded, source[:, cols], ACT.Copy, scale=gain)
+                else:
+                    scale = nc.gpsimd.tensor_scalar if engine == "gpsimd" else nc.vector.tensor_scalar
+                    scale(rounded, source[:, cols], gain, 0.0, ALU.mult, ALU.add)
+
+        def quantise_z(i, parts):
+            woven = keep.tile([P, S, PACK], BF16, name=f"z_woven{i}", align_bytes=64)
+            codes = keep.tile([P, S], U32, name=f"z_codes{i}", align_bytes=64)
+            scales = keep.tile([P, S], U8, name=f"z_scales{i}", align_bytes=64)
+            woven_words = woven[:].rearrange("p c t -> p (c t)").bitcast(F32).rearrange("p (c u) -> p c u", u=2)
+            pair_words = z_pairs[i][:].rearrange("p u c e -> p (u c e)").bitcast(F32).rearrange("p (u c) -> p c u", u=2)
+            spans = [slice(part * S // parts, (part + 1) * S // parts) for part in range(parts)]
+            for cols in spans:
+                nc.vector.tensor_copy(woven_words[:, cols, :], pair_words[:, cols, :])
+            for cols in spans:
+                nc.vector.quantize_mx(
+                    codes[:, cols].bitcast(FP8X4), scales[:, cols], woven[:, cols, :].rearrange("p c t -> p (c t)")
+                )
+            return codes, scales
+
+        z_pairs[0] = keep.tile([P, 2, S, 2], BF16, name="z_pairs0", tag=f"pair_b{PACK - 1}")
+        for t in range(PACK):
+            round_rows("gpsimd", 0, t, 1)
+        z_pairs[1] = keep.tile([P, 2, S, 2], BF16, name="z_pairs1", tag=f"placed_a{PACK - 1}")
+        z_planes = [quantise_z(0, 1)]
+        for t in range(PACK):
+            round_rows("scalar" if t < 2 else "vector", 1, t, 2 if t == PACK - 1 else 1)
+        z_planes.append(quantise_z(1, 2))
+
+        h_acc = [psum.tile([P, S], F32, name="acc") for t in range(PACK)]
+        for t in range(PACK):
+            for i, lo, hi in ((0, 0, S), (1, 0, S // 2), (1, S // 2, S)):
+                codes, scales = z_planes[i]
+                nc.tensor.matmul_mx(
+                    h_acc[t][:, lo:hi], lhsT=w_codes[:, i, 2 * P * t : 2 * P * (t + 1)].bitcast(FP4X4),
+                    lhsT_scale=w_sc[:, i, P * t : P * (t + 1)],
+                    rhs=codes[:, lo:hi].bitcast(FP8X4), rhs_scale=scales[:, lo:hi],
+                    start=(i == 0), stop=(i == 1 and hi == S),
+                )
+        h_rows = [keep.tile([P, H_WINDOW], F32, name=f"h_rows{t}") for t in range(PACK)]
+        for t in range(PACK):
+            empty = nc.scalar.copy if t % 2 == 0 else nc.vector.tensor_copy
+            empty(h_rows[t][:, 0:S], h_acc[t][:])
 
         out_rows = out_0.rearrange("(p t) j -> p t j", t=PACK)
         out_words = out_1[0].rearrange("p n t -> p (n t)").bitcast(I32)
-        o_scales = keep.tile([P, S], U8, name="o_scales", align_bytes=64)
+
+        def combine(result, chunk_start, t0, tiles, start, width, on_vector):
+            cols = slice(start, start + width)
+            entries = n5_t[:, start * MEMBERS // LIST_ROWS : (start + width) * MEMBERS // LIST_ROWS]
+            members = ring.tile([P, tiles * width, MEMBERS], F32, name="members", bufs=4)
+            spans = [slice(k * width, (k + 1) * width) for k in range(tiles)]
+            for k, span in enumerate(spans):
+                fetched = members[:, span, :].rearrange("p j e -> p (j e)")
+                if on_vector:
+                    nc.vector.tensor_copy(fetched, h_rows[t0 + k][:].indirect(entries))
+                else:
+                    nc.scalar.activation(fetched, h_rows[t0 + k][:].indirect(entries), ACT.Copy)
+            lows = ring.tile([P, tiles * width, 2], F32, name="lows")
+            highs = ring.tile([P, tiles * width, 2], F32, name="highs")
+            nc.vector.tensor_tensor(lows[:], members[:, :, 0:2], members[:, :, 2:4], ALU.min)
+            nc.vector.tensor_tensor(highs[:], members[:, :, 0:2], members[:, :, 2:4], ALU.max)
+            mn = ring.tile([P, tiles * width], F32, name="mn")
+            mx = ring.tile([P, tiles * width], F32, name="mx")
+            nc.vector.tensor_tensor(mn[:], lows[:, :, 0], lows[:, :, 1], ALU.min)
+            nc.vector.tensor_tensor(mx[:], highs[:, :, 0], highs[:, :, 1], ALU.max)
+            top = ring.tile([P, tiles * width], F32, name="top")
+            for k, span in enumerate(spans):
+                nc.vector.tensor_tensor(top[:, span], mn[:, span], h_rows[t0 + k][:, cols], ALU.max)
+            done = result[:, t0 : t0 + tiles, start - chunk_start : start - chunk_start + width]
+            nc.vector.scalar_tensor_tensor(
+                done, mx[:].rearrange("p (t j) -> p t j", t=tiles), -0.5,
+                top[:].rearrange("p (t j) -> p t j", t=tiles), ALU.mult, ALU.add,
+            )
+            nc.sync.dma_start(out_rows[:, t0 : t0 + tiles, cols], done)
+
         wovens = []
-        for c, CHUNK in enumerate(CHUNKS):
-            first = sum(CHUNKS[:c])
-            cols = slice(first, first + CHUNK)
-            result = keep.tile([P, PACK, CHUNK], F32, name=f"result{c}")
-            for t in range(PACK):
-                members = ring.tile([P, CHUNK, 4], F32, name="members", bufs=4)
-                lo, hi = first * 4 // 16, (first + CHUNK) * 4 // 16
-                nc.scalar.activation(
-                    members[:].rearrange("p j e -> p (j e)"), h_rows[t][:].indirect(n5_t[:, lo:hi]), ACT.Copy
-                )
-                lows = ring.tile([P, CHUNK, 2], F32, name="lows")
-                highs = ring.tile([P, CHUNK, 2], F32, name="highs")
-                nc.vector.tensor_tensor(lows[:], members[:, :, 0:2], members[:, :, 2:4], ALU.min)
-                nc.vector.tensor_tensor(highs[:], members[:, :, 0:2], members[:, :, 2:4], ALU.max)
-                mn = ring.tile([P, CHUNK], F32, name="mn")
-                mx = ring.tile([P, CHUNK], F32, name="mx")
-                nc.vector.tensor_tensor(mn[:], lows[:, :, 0], lows[:, :, 1], ALU.min)
-                nc.vector.tensor_tensor(mx[:], highs[:, :, 0], highs[:, :, 1], ALU.max)
-                top = ring.tile([P, CHUNK], F32, name="top")
-                nc.vector.tensor_tensor(top[:], mn[:], h_rows[t][:, cols], ALU.max)
-                nc.vector.scalar_tensor_tensor(result[:, t, :], mx[:], -0.5, top[:], ALU.mult, ALU.add)
-                nc.sync.dma_start(out_rows[:, t, cols], result[:, t, :])
-            woven = keep.tile([P, CHUNK * PACK], BF16, name=f"o_woven{c}", align_bytes=64)
+        for c, width in enumerate(CHUNKS):
+            start = sum(CHUNKS[:c])
+            result = keep.tile([P, PACK, width], F32, name=f"result{c}")
+            tiles = PIECE // width
+            for t0 in range(0, PACK, tiles):
+                if c == 0 and t0 == 0:
+                    combine(result, start, 1, 1, start, width // 2, True)
+                if c == 0 and t0 == 1:
+                    combine(result, start, 1, 1, start + width // 2, width // 2, False)
+                else:
+                    combine(result, start, t0, tiles, start, width, False)
+            woven = keep.tile([P, width * PACK], BF16, name=f"o_woven{c}", align_bytes=64)
             weave = nc.vector.tensor_copy if c == len(CHUNKS) - 1 else nc.scalar.copy
             weave(
                 woven[:].rearrange("p (c i t) -> p c t i", i=4, t=PACK),
                 result[:].rearrange("p t (c i) -> p c t i", i=4),
             )
-            wovens.append((cols, woven))
+            wovens.append((slice(start, start + width), woven))
+
+        o_scales = keep.tile([P, S], U8, name="o_scales", align_bytes=64)
         for c, (cols, woven) in enumerate(wovens):
             o_codes = keep.tile([P, CHUNKS[c]], U32, name=f"o_codes{c}", align_bytes=64)
             nc.vector.quantize_mx(o_codes[:].bitcast(FP8X4), o_scales[:, cols], woven[:])
             nc.sync.dma_start(out_words[:, cols], o_codes[:].bitcast(I32))
-        for q in range(4):
+        for q in range(QUADS):
             queue = nc.sync if q % 2 == 0 else nc.scalar
-            queue.dma_start(out_2[0, 4 * q : 4 * q + 4, :].bitcast(I32), o_scales[32 * q : 32 * q + 4, :].bitcast(I32))
+            queue.dma_start(
+                out_2[0, PACK * q : PACK * (q + 1), :].bitcast(I32), o_scales[32 * q : 32 * q + PACK, :].bitcast(I32)
+            )

from contextlib import ExitStack

import concourse.mybir as mybir

K, T, S, N, G, H, W = 512, 1024, 512, 512, 2048, 512, 256
FLOPS = 2 * K * H * S * 2 + 2 * H * N * S * 2

F32 = mybir.dt.float32
BF16 = mybir.dt.bfloat16
I32 = mybir.dt.int32
U32 = mybir.dt.uint32
U16 = mybir.dt.uint16
U8 = mybir.dt.uint8
FP8X4 = mybir.dt.float8_e4m3fn_x4
FP4X4 = mybir.dt.float4_e2m1fn_x4
ALU = mybir.AluOpType
ACT = mybir.ActivationFunctionType

P = 128
PACK = 4
QUADS = 4
BLOCK_PARTS = 8
LIST_ROWS = 16
MEMBERS = 4
SCORE_SCALE = 0.0625
PIECE = 256
CHUNKS = (256, 128, 128)
H_WINDOW = MEMBERS * PIECE + 64


def tile_picked_kjbondduelgmid_none_po_kernel(
    tc, x_words, x_scales, d_words, d_scales, gn, gm, w1_words, w1_scales, w2_words, w2_scales,
    offs, k1, two, n1, n2, n3, n4, n5, out_0, out_1, out_2,
):
    nc = tc.nc
    with ExitStack() as ctx:
        lists = ctx.enter_context(tc.tile_pool(name="lists", bufs=1))
        keep = ctx.enter_context(tc.tile_pool(name="keep", bufs=1))
        ring = ctx.enter_context(tc.tile_pool(name="ring", bufs=3))
        psum = ctx.enter_context(tc.psum_pool(name="psum", bufs=2 * PACK))

        def load_list(src, name):
            tile = lists.tile(list(src.shape), U16, name=name)
            nc.sync.dma_start(tile[:], src)
            return tile

        def deal(engine_copy, dealt, plain):
            engine_copy(dealt, plain.rearrange("p (m t) -> p t m", t=PACK))

        def place_scale_rows(plane, dealt, first):
            for q in range(QUADS):
                nc.sync.dma_start(
                    plane[32 * q : 32 * q + PACK, :].bitcast(I32),
                    dealt[32 * q + first : 32 * (q + 1) : BLOCK_PARTS, :].bitcast(I32),
                )

        d_sc_table = keep.tile([P, G], U8, name="d_sc_table")
        nc.gpsimd.memset(d_sc_table[:].bitcast(I32), 0)
        nc.sync.dma_start(d_sc_table[0:P:BLOCK_PARTS, :].bitcast(I32), d_scales[0].bitcast(I32))
        x_sc_table = keep.tile([P, T], U8, name="x_sc_table")
        nc.gpsimd.memset(x_sc_table[:].bitcast(I32), 0)
        k1_t = load_list(k1, "k1_t")
        offs_t = load_list(offs, "offs_t")
        d_table = keep.tile([P, G], I32, name="d_table")
        nc.sync.dma_start(d_table[:], d_words[0].rearrange("p n t -> p (n t)").bitcast(I32))
        for q in range(QUADS):
            nc.sync.dma_start(
                x_sc_table[32 * q : 32 * q + PACK, :].bitcast(I32), x_scales[0, PACK * q : PACK * (q + 1), :].bitcast(I32)
            )
        x_table = keep.tile([P, T], I32, name="x_table")
        nc.sync.dma_start(x_table[:], x_words[0].rearrange("p n t -> p (n t)").bitcast(I32))
        n1_t = load_list(n1, "n1_t")
        n2_t = load_list(n2, "n2_t")

        key_scales = keep.tile([P, H], U8, name="key_scales", align_bytes=64)
        nc.vector.memset(key_scales[:].bitcast(I32), 0)

        warm = keep.tile([P, 2, 8], F32, name="warm")
        nc.vector.memset(warm[:, 0, :], 0.0)
        nc.scalar.activation(warm[:, 1, :], warm[:, 0, :], ACT.Sigmoid)

        d_sc_dealt = keep.tile([P, H], U8, name="d_sc_dealt", tag="stage2", align_bytes=64)
        half_cols = H // 2 // LIST_ROWS
        d_sc_halves = []
        for half in range(2):
            picked = keep.tile([P, H // 2], U8, name=f"d_sc_picked{half}", tag=f"stage{half}", align_bytes=64)
            nc.vector.tensor_copy(
                picked[:], d_sc_table[:].indirect(k1_t[:, half_cols * half : half_cols * (half + 1)])
            )
            d_sc_halves.append(picked)
        for half in range(2):
            places = d_sc_dealt[:].rearrange("p (t m) -> p t m", t=PACK)[:, :, P // 2 * half : P // 2 * (half + 1)]
            deal(nc.vector.tensor_copy, places, d_sc_halves[half][:])
        place_scale_rows(key_scales, d_sc_dealt, 0)
        two_t = load_list(two, "two_t")
        n3_t = load_list(n3, "n3_t")
        n4_t = load_list(n4, "n4_t")
        n5_t = load_list(n5, "n5_t")

        def pick_words(offsets, name, tag):
            words = keep.tile([P, S], U32, name=name, tag=tag, align_bytes=64)
            nc.vector.tensor_copy(words[:], x_table[:].bitcast(U32).indirect(offsets[:]))
            return words

        def pick_scales(offsets, name, tag):
            scales = keep.tile([P, S], U8, name=name, tag=tag, align_bytes=64)
            nc.vector.tensor_copy(scales[:], x_sc_table[:].indirect(offsets[:]))
            return scales

        d_picked = keep.tile([P, H], U32, name="d_picked", tag="stage1", align_bytes=64)
        nc.vector.tensor_copy(d_picked[:], d_table[:].bitcast(U32).indirect(k1_t[:]))
        key_words = keep.tile([P, H], I32, name="key_words", align_bytes=64)
        deal(nc.vector.tensor_copy, key_words[:].rearrange("p (t m) -> p t m", t=PACK), d_picked[:].bitcast(I32))
        xa_scales = pick_scales(offs_t, "xa_scales", "stage0")
        xa_words = pick_words(offs_t, "xa_words", "xa_words")

        def score(words, scales, t):
            acc = psum.tile([P, S], F32, name="acc")
            cols = slice(P * t, P * (t + 1))
            nc.tensor.matmul_mx(
                acc[:], lhsT=key_words[:, cols].bitcast(FP8X4), lhsT_scale=key_scales[:, cols],
                rhs=words[:].bitcast(FP8X4), rhs_scale=scales[:], start=True, stop=True,
            )
            return acc

        a_acc = [score(xa_words, xa_scales, t) for t in range(PACK)]
        xb_words = pick_words(two_t, "xb_words", "stage1")
        xb_scales = pick_scales(two_t, "xb_scales", "stage2")
        b_acc = [score(xb_words, xb_scales, t) for t in range(PACK)]

        w_raw = keep.tile([P, 2, 2 * N], U8, name="w_raw")
        for i, words in enumerate((w1_words, w2_words)):
            nc.gpsimd.dma_start(w_raw[:, i, :].bitcast(I32), words[0].bitcast(I32))
        w_sc_raw = keep.tile([P, N], U8, name="w_sc_raw")
        nc.vector.memset(w_sc_raw[:].bitcast(I32), 0)
        for i, scales in enumerate((w1_scales, w2_scales)):
            nc.gpsimd.dma_start(w_sc_raw[i:P:BLOCK_PARTS, :].bitcast(I32), scales[0].bitcast(I32))
        gains = keep.tile([P, 2, 8], F32, name="gains")
        for i, gain in enumerate((gn, gm)):
            nc.gpsimd.dma_start(gains[:, i, 0:PACK], gain.rearrange("(p t) o -> p (t o)", t=PACK))
        w_codes = keep.tile([P, 2, 2 * N], U8, name="w_codes", align_bytes=64)
        nc.scalar.copy(
            w_codes[:].bitcast(U16).rearrange("p i (t m) -> p i t m", t=PACK),
            w_raw[:].bitcast(U16).rearrange("p i (m t) -> p i t m", t=PACK),
        )

        accs = {"a": a_acc, "b": b_acc}
        pair_lists = {"a": (n1_t, n2_t), "b": (n3_t, n4_t)}
        rows, pair, placed, diff, gated = {}, {}, {}, {}, {}

        def empty_bank(kind, t):
            name = f"rows_{kind}{t}"
            rows[kind, t] = keep.tile([P, S], F32, name=name, tag=name)
            if (kind, t) == ("a", 1):
                nc.vector.tensor_scalar(rows[kind, t][:], accs[kind][t][:], SCORE_SCALE, None, ALU.mult)
            else:
                nc.scalar.activation(rows[kind, t][:], accs[kind][t][:], ACT.Copy, scale=SCORE_SCALE)

        def pick_pair(kind, t):
            name = f"pair_{kind}{t}"
            pair[kind, t] = keep.tile([P, 2, W], F32, name=name, tag=name)
            for side in range(2):
                nc.scalar.activation(
                    pair[kind, t][:, side, :], rows[kind, t][:].indirect(pair_lists[kind][side][:]), ACT.Copy
                )

        def place_sum(t):
            placed["a", t] = keep.tile([P, S], F32, name=f"placed_a{t}", tag=f"placed_a{t}")
            window, pa, pb = placed["a", t][:].indirect(n1_t[:]), pair["a", t][:, 0, :], pair["a", t][:, 1, :]
            if t == 0:
                nc.vector.tensor_tensor(window, pa, pb, ALU.add)
            else:
                total = ring.tile([P, W], F32, name="total")
                nc.gpsimd.tensor_tensor(total[:], pa, pb, ALU.add)
                nc.vector.tensor_copy(window, total[:])

        def place_product(t):
            tag = f"rows_a{t + 1}" if t % 2 == 0 else f"product{t}"
            product = keep.tile([P, W], F32, name=f"product{t}", tag=tag)
            nc.gpsimd.tensor_tensor(product[:], pair["a", t][:, 0, :], pair["a", t][:, 1, :], ALU.mult)
            nc.vector.tensor_copy(placed["a", t][:].indirect(n2_t[:]), product[:])

        def subtract(t):
            diff[t] = keep.tile([P, W], F32, name=f"diff{t}", tag=f"diff{t}")
            nc.gpsimd.tensor_tensor(diff[t][:], pair["b", t][:, 0, :], pair["b", t][:, 1, :], ALU.subtract)

        def gate(t):
            sigmoids = ring.tile([P, 2, W], F32, name="sigmoids")
            for side, sign in enumerate((1.0, -1.0)):
                nc.scalar.activation(sigmoids[:, side, :], diff[t][:], ACT.Sigmoid, scale=sign)
            gated[t] = keep.tile([P, 2, W], F32, name=f"gated{t}")
            nc.gpsimd.tensor_tensor(gated[t][:], pair["b", t][:], sigmoids[:], ALU.mult)

        def place_gated(t, tag):
            placed["b", t] = keep.tile([P, S], F32, name=f"placed_b{t}", tag=tag)
            for side in range(2):
                window = placed["b", t][:].indirect(pair_lists["b"][side][:])
                if t % 2 == 0:
                    nc.vector.tensor_copy(window, gated[t][:, side, :])
                else:
                    nc.scalar.activation(window, gated[t][:, side, :], ACT.Copy)

        turns = [("a", 0), ("a", 1), ("b", 0), ("a", 2), ("a", 3), ("b", 1), ("b", 2), ("b", 3)]
        for kind, t in turns:
            empty_bank(kind, t)
            pick_pair(kind, t)
            if kind == "b":
                subtract(t)
                continue
            place_sum(t)
            if t % 2 == 1:
                place_product(t - 1)
                place_product(t)
            if t == PACK - 1:
                gate(0)
        for t in range(1, PACK):
            gate(t)
        place_gated(0, f"product{PACK - 1}")
        place_gated(2, "placed_b2")
        place_gated(1, f"diff{PACK - 1}")
        place_gated(3, "placed_b3")

        w_sc_dealt = keep.tile([P, N], U8, name="w_sc_dealt", tag="rows_a0")
        deal(nc.vector.tensor_copy, w_sc_dealt[:].rearrange("p (t m) -> p t m", t=PACK), w_sc_raw[:])
        w_sc = keep.tile([P, 2, N], U8, name="w_sc", align_bytes=64)
        nc.vector.memset(w_sc[:].rearrange("p i n -> p (i n)").bitcast(I32), 0)
        for i in range(2):
            place_scale_rows(w_sc[:, i, :], w_sc_dealt, i)

        z_pairs = {}

        def round_rows(engine, i, t, parts):
            source = placed["ab"[i], t]
            for part in range(parts):
                cols = slice(part * S // parts, (part + 1) * S // parts)
                rounded, gain = z_pairs[i][:, t // 2, cols, t % 2], gains[:, i, t : t + 1]
                if engine == "scalar":
                    nc.scalar.activation(rounded, source[:, cols], ACT.Copy, scale=gain)
                else:
                    scale = nc.gpsimd.tensor_scalar if engine == "gpsimd" else nc.vector.tensor_scalar
                    scale(rounded, source[:, cols], gain, 0.0, ALU.mult, ALU.add)

        def quantise_z(i, parts):
            woven = keep.tile([P, S, PACK], BF16, name=f"z_woven{i}", align_bytes=64)
            codes = keep.tile([P, S], U32, name=f"z_codes{i}", align_bytes=64)
            scales = keep.tile([P, S], U8, name=f"z_scales{i}", align_bytes=64)
            woven_words = woven[:].rearrange("p c t -> p (c t)").bitcast(F32).rearrange("p (c u) -> p c u", u=2)
            pair_words = z_pairs[i][:].rearrange("p u c e -> p (u c e)").bitcast(F32).rearrange("p (u c) -> p c u", u=2)
            spans = [slice(part * S // parts, (part + 1) * S // parts) for part in range(parts)]
            for cols in spans:
                nc.vector.tensor_copy(woven_words[:, cols, :], pair_words[:, cols, :])
            for cols in spans:
                nc.vector.quantize_mx(
                    codes[:, cols].bitcast(FP8X4), scales[:, cols], woven[:, cols, :].rearrange("p c t -> p (c t)")
                )
            return codes, scales

        z_pairs[0] = keep.tile([P, 2, S, 2], BF16, name="z_pairs0", tag=f"pair_b{PACK - 1}")
        for t in range(PACK):
            round_rows("gpsimd", 0, t, 1)
        z_pairs[1] = keep.tile([P, 2, S, 2], BF16, name="z_pairs1", tag=f"placed_a{PACK - 1}")
        z_planes = [quantise_z(0, 1)]
        for t in range(PACK):
            round_rows("scalar" if t < 2 else "vector", 1, t, 2 if t == PACK - 1 else 1)
        z_planes.append(quantise_z(1, 2))

        h_acc = [psum.tile([P, S], F32, name="acc") for t in range(PACK)]
        for t in range(PACK):
            for i, lo, hi in ((0, 0, S), (1, 0, S // 2), (1, S // 2, S)):
                codes, scales = z_planes[i]
                nc.tensor.matmul_mx(
                    h_acc[t][:, lo:hi], lhsT=w_codes[:, i, 2 * P * t : 2 * P * (t + 1)].bitcast(FP4X4),
                    lhsT_scale=w_sc[:, i, P * t : P * (t + 1)],
                    rhs=codes[:, lo:hi].bitcast(FP8X4), rhs_scale=scales[:, lo:hi],
                    start=(i == 0), stop=(i == 1 and hi == S),
                )
        h_rows = [keep.tile([P, H_WINDOW], F32, name=f"h_rows{t}") for t in range(PACK)]
        for t in range(PACK):
            empty = nc.scalar.copy if t % 2 == 0 else nc.vector.tensor_copy
            empty(h_rows[t][:, 0:S], h_acc[t][:])

        out_rows = out_0.rearrange("(p t) j -> p t j", t=PACK)
        out_words = out_1[0].rearrange("p n t -> p (n t)").bitcast(I32)

        def combine(result, chunk_start, t0, tiles, start, width, on_vector):
            cols = slice(start, start + width)
            entries = n5_t[:, start * MEMBERS // LIST_ROWS : (start + width) * MEMBERS // LIST_ROWS]
            members = ring.tile([P, tiles * width, MEMBERS], F32, name="members", bufs=4)
            spans = [slice(k * width, (k + 1) * width) for k in range(tiles)]
            for k, span in enumerate(spans):
                fetched = members[:, span, :].rearrange("p j e -> p (j e)")
                if on_vector:
                    nc.vector.tensor_copy(fetched, h_rows[t0 + k][:].indirect(entries))
                else:
                    nc.scalar.activation(fetched, h_rows[t0 + k][:].indirect(entries), ACT.Copy)
            lows = ring.tile([P, tiles * width, 2], F32, name="lows")
            highs = ring.tile([P, tiles * width, 2], F32, name="highs")
            nc.vector.tensor_tensor(lows[:], members[:, :, 0:2], members[:, :, 2:4], ALU.min)
            nc.vector.tensor_tensor(highs[:], members[:, :, 0:2], members[:, :, 2:4], ALU.max)
            mn = ring.tile([P, tiles * width], F32, name="mn")
            mx = ring.tile([P, tiles * width], F32, name="mx")
            nc.vector.tensor_tensor(mn[:], lows[:, :, 0], lows[:, :, 1], ALU.min)
            nc.vector.tensor_tensor(mx[:], highs[:, :, 0], highs[:, :, 1], ALU.max)
            top = ring.tile([P, tiles * width], F32, name="top")
            for k, span in enumerate(spans):
                nc.vector.tensor_tensor(top[:, span], mn[:, span], h_rows[t0 + k][:, cols], ALU.max)
            done = result[:, t0 : t0 + tiles, start - chunk_start : start - chunk_start + width]
            nc.vector.scalar_tensor_tensor(
                done, mx[:].rearrange("p (t j) -> p t j", t=tiles), -0.5,
                top[:].rearrange("p (t j) -> p t j", t=tiles), ALU.mult, ALU.add,
            )
            nc.sync.dma_start(out_rows[:, t0 : t0 + tiles, cols], done)

        wovens = []
        for c, width in enumerate(CHUNKS):
            start = sum(CHUNKS[:c])
            result = keep.tile([P, PACK, width], F32, name=f"result{c}")
            tiles = PIECE // width
            for t0 in range(0, PACK, tiles):
                if c == 0 and t0 == 0:
                    combine(result, start, 1, 1, start, width // 2, True)
                if c == 0 and t0 == 1:
                    combine(result, start, 1, 1, start + width // 2, width // 2, False)
                else:
                    combine(result, start, t0, tiles, start, width, False)
            woven = keep.tile([P, width * PACK], BF16, name=f"o_woven{c}", align_bytes=64)
            weave = nc.vector.tensor_copy if c == len(CHUNKS) - 1 else nc.scalar.copy
            weave(
                woven[:].rearrange("p (c i t) -> p c t i", i=4, t=PACK),
                result[:].rearrange("p t (c i) -> p c t i", i=4),
            )
            wovens.append((slice(start, start + width), woven))

        o_scales = keep.tile([P, S], U8, name="o_scales", align_bytes=64)
        for c, (cols, woven) in enumerate(wovens):
            o_codes = keep.tile([P, CHUNKS[c]], U32, name=f"o_codes{c}", align_bytes=64)
            nc.vector.quantize_mx(o_codes[:].bitcast(FP8X4), o_scales[:, cols], woven[:])
            nc.sync.dma_start(out_words[:, cols], o_codes[:].bitcast(I32))
        for q in range(QUADS):
            queue = nc.sync if q % 2 == 0 else nc.scalar
            queue.dma_start(
                out_2[0, PACK * q : PACK * (q + 1), :].bitcast(I32), o_scales[32 * q : 32 * q + PACK, :].bitcast(I32)
            )
